import numpy as np, ml_dtypes
CORES = [9,10,11,14,17,18,19,22,49,50,51,54]
N = 12
import mx_ref
NC = 128
BF = ml_dtypes.bfloat16
def setup_inputs(rng):
    def f(*shape):
        return mx_ref.flush((rng.standard_normal(shape, dtype=np.float32) * np.exp2(rng.integers(-2, 3, shape[:-1] + (1,)))).astype(BF))
    return {"w": f(N, 128, 512), "x": f(N, 128, N * 4 * NC)}
def setup_inputs_blocks(rng):
    d = setup_inputs(rng)
    for k in ("w", "x"): d[k] = mx_ref.spread(d[k], rng, 4)
    return d
def setup_inputs_wide(rng):
    d = setup_inputs(rng)
    for k in ("w", "x"): d[k] = mx_ref.flush((d[k].astype(np.float32) * np.exp2(rng.integers(-8, 9, (N, 1, 1))).astype(np.float32)).astype(BF))
    return d
def setup_inputs_zeros(rng):
    d = setup_inputs(rng); v = d["x"].reshape(N, 128, -1, 4).copy()
    v[np.broadcast_to((rng.random((N, 1, v.shape[2], 1)) < 0.33), v.shape)] = 0
    d["x"] = v.reshape(d["x"].shape)
    return d
def reference(w, x):
    y = np.zeros((N, 128, N * NC), np.float32)
    for r in range(N):
        qw = mx_ref.quantize(w[r])
        for j in range(N):
            y[r][:, NC * j:NC * j + NC] = mx_ref.matmul(qw, mx_ref.quantize(x[j][:, 4 * NC * r:4 * NC * r + 4 * NC]))
    return {"y": y}

@@ -1,0 +1,197 @@
+from concourse.bass import DstId, RemoteDMATransfer
+from concourse.mybir import dt
+
+N = 12
+SIM = 64
+TW = 128
+BANK = 512
+NP = 5
+
+SCRATCH = {
+    "xb": ("sbuf", [128, N * 4 * TW], "bfloat16"),
+    "wb": ("sbuf", [128, 4 * TW], "bfloat16"),
+    "xq": ("sbuf", [128, N * TW], "float8_e4m3fn_x4"),
+    "xs": ("sbuf", [128, N * TW], "uint8"),
+    "wq": ("sbuf", [128, TW], "float8_e4m3fn_x4"),
+    "ws": ("sbuf", [128, TW], "uint8"),
+    "lq": ("sbuf", [128, N * TW], "float8_e4m3fn_x4"),
+    "ls": ("sbuf", [128, N * TW], "uint8"),
+    "ps": ("psum", [128, NP * BANK], "float32"),
+    "yb": ("sbuf", [128, N * TW], "float32"),
+}
+SEMAPHORES = (["ld0", "ld1", "ld2", "ldw", "q0", "q1", "q2", "qo", "qw", "st0", "st1", "sent", "hc0", "hc1", "hs"]
+              + ["arr%d" % j for j in range(N)] + ["mm%d" % k for k in range(NP)] + ["ev%d" % k for k in range(NP)])
+
+
+def engines(mask):
+    return [e for e in range(mask.bit_length()) if (mask >> e) & 1]
+
+
+def split(engs, k):
+    per = 1
+    while per * 2 * k <= len(engs):
+        per *= 2
+    return [engs[i * per:(i + 1) * per] for i in range(k)]
+
+
+def build(T, topo):
+    cores = list(T.cores)
+    chips = []
+    for c in cores:
+        if topo.chip(c) not in chips:
+            chips.append(topo.chip(c))
+    members = {ch: [r for r, c in enumerate(cores) if topo.chip(c) == ch] for ch in chips}
+
+    def after(ch):
+        i = chips.index(ch)
+        return [chips[(i + k) % len(chips)] for k in range(1, len(chips))]
+
+    def reaches(h, D):
+        return all(topo.may_write(h, cores[r]) for r in members[D])
+
+    idle = [h for h in range(SIM) if h not in cores]
+    blocked = [any(not topo.may_write(c, d) for d in cores if d != c) for c in cores]
+    route, jobs = {}, {}
+    for s, c in enumerate(cores):
+        if blocked[s]:
+            ch = topo.chip(c)
+            spare = [h for h in idle if topo.chip(h) == ch and topo.die(h) != topo.die(c)]
+            opts = {D: [h for h in spare if reaches(h, D)] for D in after(ch)}
+            used = []
+            for D in sorted(after(ch), key=lambda D: len(opts[D])):
+                fresh = [h for h in opts[D] if h not in used]
+                route[(s, D)] = (fresh or opts[D])[0]
+                used.append(route[(s, D)])
+            for D in after(ch):
+                jobs.setdefault(route[(s, D)], []).append((s, D))
+
+    prog = {}
+
+    def to_ranks(what, s, ranks, sets):
+        return [(cores[r], e, "arr%d" % s, what, r, "l", s, 1) for r, e in zip(ranks, sets)]
+
+    for s, c in enumerate(cores):
+        ch = topo.chip(c)
+        A, B = after(ch)
+        peers = [r for r in members[ch] if r != s]
+        on = engines(topo.mask(c, cores[peers[0]]))
+        if not blocked[s]:
+            off = engines(topo.mask(c, cores[members[A][0]]))
+            near = [e for e in on if e not in off]
+            both = members[A] + members[B]
+            prog[c] = [
+                (["q0"], to_ranks("c", s, members[A], split(off, len(members[A])))),
+                (["q1", "q2"], to_ranks("s", s, both, split(off, len(both)))
+                 + to_ranks("s", s, peers, split(near, len(peers)))),
+                ([], to_ranks("c", s, members[B], split(off, len(members[B])))
+                 + to_ranks("c", s, peers, split(near, len(peers)))),
+            ]
+        else:
+            far, near = on[:len(on) // 2], on[len(on) // 2:]
+
+            def hand(what, D, e):
+                h = route[(s, D)]
+                sem = "hs" if what == "s" else "hc%d" % jobs[h].index((s, D))
+                return (h, e, sem, what, members[D][0], "x", members[D][0], len(members[D]))
+            two = split(far, 2)
+            prog[c] = [
+                (["q0"], [hand("c", A, far)]),
+                (["q1"], [hand("c", B, far)]),
+                (["q2"], [hand("s", A, two[0]), hand("s", B, two[1])]
+                 + to_ranks("c", s, peers, split(near, len(peers)))),
+                ([], to_ranks("s", s, peers, split(near, len(peers)))),
+            ]
+    for h, todo in jobs.items():
+        off = engines(topo.mask(h, cores[members[todo[0][1]][0]]))
+        every = [(s, r) for s, D in todo for r in members[D]]
+        calls = [(["hc0"], to_ranks("c", todo[0][0], members[todo[0][1]], split(off, len(members[todo[0][1]])))),
+                 (["hs"], [to_ranks("s", s, [r], [e])[0] for (s, r), e in zip(every, split(off, len(every)))])]
+        for i, (s, D) in enumerate(todo[1:]):
+            calls.append((["hc%d" % (i + 1)], to_ranks("c", s, members[D], split(off, len(members[D])))))
+        prog[h] = calls
+
+    inc = {}
+    for c, calls in prog.items():
+        for waits, trs in calls:
+            for tr in trs:
+                inc[(tr[0], tr[2])] = inc.get((tr[0], tr[2]), 0) + len(tr[1])
+    return cores, members, after, blocked, prog, inc
+
+
+def rank_program(g, core, T, topo):
+    cores, members, after, blocked, prog, inc = build(T, topo)
+    if core not in prog:
+        return
+    me = T.rank_of(core)
+
+    def cols(b, n=1, f=1):
+        return slice(b * TW * f, (b + n) * TW * f)
+
+    sent = 0
+    for waits, trs in prog[core]:
+        for name in waits:
+            g.wait_ge(T.sem[name], inc.get((core, name), 1))
+        call = []
+        for dst, engs, sem, what, sb, land, lb, n in trs:
+            rid, pid = topo.addr(dst)[:2]
+            mask = 0
+            for e in engs:
+                mask |= 1 << e
+            if what == "c":
+                src = T.xq[:, cols(sb, n)].bitcast(dt.uint8)
+                out = (T.lq if land == "l" else T.xq)[:, cols(lb, n)].bitcast(dt.uint8)
+            else:
+                src = T.xs[:, cols(sb, n)]
+                out = (T.ls if land == "l" else T.xs)[:, cols(lb, n)]
+            call.append(RemoteDMATransfer(dst_ids=[DstId(rid=rid, pnc=pid)], dma_engine_mask=mask,
+                                          remote_sem=T.sem[sem], src=src, dst=out))
+            sent += len(engs)
+        g.remote_dma_fused(call, local_sem=T.sem.sent)
+    g.wait_ge(T.sem.sent, sent)
+    if me is None:
+        return
+
+    ch = topo.chip(core)
+    order = after(ch) + [ch]
+    queues = [g.sync, g.scalar]
+    for i, D in enumerate(order):
+        b, n = members[D][0], len(members[D])
+        queues[i % 2].dma_start(T.xb[:, cols(b, n, 4)], T.x[:, cols(b, n, 4)]).then_inc(T.sem["ld%d" % i], 16)
+    queues[len(order) % 2].dma_start(T.wb[:], T.w[:]).then_inc(T.sem.ldw, 16)
+
+    for i, D in enumerate(order):
+        b, n = members[D][0], len(members[D])
+        g.vector.wait_ge(T.sem["ld%d" % i], 16)
+        g.vector.quantize_mx(T.xq[:, cols(b, n)], T.xs[:, cols(b, n)], T.xb[:, cols(b, n, 4)]).then_inc(T.sem["q%d" % i], 1)
+    g.vector.quantize_mx(T.lq[:, cols(me)], T.ls[:, cols(me)], T.xb[:, cols(me, 1, 4)]).then_inc(T.sem.qo, 1)
+    g.vector.wait_ge(T.sem.ldw, 16)
+    g.vector.quantize_mx(T.wq[:], T.ws[:], T.wb[:]).then_inc(T.sem.qw, 1)
+
+    pieces = [(members[ch][0], len(members[ch]))]
+    for P in reversed(after(ch)):
+        runs = []
+        for j in members[P]:
+            if runs and blocked[runs[-1][0]] == blocked[j] and runs[-1][0] + runs[-1][1] == j:
+                runs[-1] = (runs[-1][0], runs[-1][1] + 1)
+            else:
+                runs.append((j, 1))
+        pieces += sorted(runs, key=lambda r: blocked[r[0]])
+
+    g.tensor.wait_ge(T.sem.qw, 1)
+    stored = [0, 0]
+    for k, (j0, n) in enumerate(pieces):
+        for j in range(j0, j0 + n):
+            if j == me:
+                g.tensor.wait_ge(T.sem.qo, 1)
+            else:
+                g.tensor.wait_ge(T.sem["arr%d" % j], inc[(core, "arr%d" % j)])
+        bank = T.ps[:, k * BANK:k * BANK + n * TW]
+        g.tensor.matmul_mx(bank, T.wq[:], T.ws[:], T.lq[:, cols(j0, n)], T.ls[:, cols(j0, n)], True, True).then_inc(T.sem["mm%d" % k], 1)
+        g.vector.wait_ge(T.sem["mm%d" % k], 1)
+        g.vector.tensor_copy(T.yb[:, cols(j0, n)], bank).then_inc(T.sem["ev%d" % k], 1)
+        q = queues[k % 2]
+        q.wait_ge(T.sem["ev%d" % k], 1)
+        q.dma_start(T.y[:, cols(j0, n)], T.yb[:, cols(j0, n)]).then_inc(T.sem["st%d" % (k % 2)], 16)
+        stored[k % 2] += 16
+    for i, q in enumerate(queues):
+        q.wait_ge(T.sem["st%d" % i], stored[i])

@@ -5,13 +5,16 @@ N = 12
 SIM = 64
 TW = 128
 BANK = 512
-NP = 5
+NP = 7
+NL = 4
 
 SCRATCH = {
     "xb": ("sbuf", [128, N * 4 * TW], "bfloat16"),
     "wb": ("sbuf", [128, 4 * TW], "bfloat16"),
     "xq": ("sbuf", [128, N * TW], "float8_e4m3fn_x4"),
     "xs": ("sbuf", [128, N * TW], "uint8"),
+    "hq": ("sbuf", [128, N * TW], "float8_e4m3fn_x4"),
+    "hp": ("sbuf", [128, N * TW], "uint8"),
     "wq": ("sbuf", [128, TW], "float8_e4m3fn_x4"),
     "ws": ("sbuf", [128, TW], "uint8"),
     "lq": ("sbuf", [128, N * TW], "float8_e4m3fn_x4"),
@@ -19,7 +22,8 @@ SCRATCH = {
     "ps": ("psum", [128, NP * BANK], "float32"),
     "yb": ("sbuf", [128, N * TW], "float32"),
 }
-SEMAPHORES = (["ld0", "ld1", "ld2", "ldw", "q0", "q1", "q2", "qo", "qw", "st0", "st1", "sent", "hc0", "hc1", "hs"]
+SEMAPHORES = (["ldw", "qo", "qw", "st0", "st1", "sent", "hc0", "hc1", "hs"]
+              + ["ld%d" % i for i in range(NL)] + ["q%d" % i for i in range(NL)]
               + ["arr%d" % j for j in range(N)] + ["mm%d" % k for k in range(NP)] + ["ev%d" % k for k in range(NP)])
 
 
@@ -51,78 +55,108 @@ def build(T, topo):
 
     idle = [h for h in range(SIM) if h not in cores]
     blocked = [any(not topo.may_write(c, d) for d in cores if d != c) for c in cores]
-    route, jobs = {}, {}
-    for s, c in enumerate(cores):
-        if blocked[s]:
-            ch = topo.chip(c)
-            spare = [h for h in idle if topo.chip(h) == ch and topo.die(h) != topo.die(c)]
-            opts = {D: [h for h in spare if reaches(h, D)] for D in after(ch)}
-            used = []
-            for D in sorted(after(ch), key=lambda D: len(opts[D])):
-                fresh = [h for h in opts[D] if h not in used]
-                route[(s, D)] = (fresh or opts[D])[0]
-                used.append(route[(s, D)])
-            for D in after(ch):
-                jobs.setdefault(route[(s, D)], []).append((s, D))
+    kind = ["hand" if b else "direct" for b in blocked]
+    route, used = {}, []
+
+    def pick(s, D, opts):
+        route[(s, D)] = [h for h in opts if h not in used][0]
+        used.append(route[(s, D)])
+
+    for ch in chips:
+        leaves = {}
+        for s in members[ch]:
+            if blocked[s]:
+                other = [topo.die(h) for h in idle if topo.chip(h) == ch and topo.die(h) != topo.die(cores[s])][0]
+                leaves.setdefault(other, []).append(s)
+        for s in members[ch]:
+            if not blocked[s]:
+                leaves.setdefault(topo.die(cores[s]), []).append(s)
+        for d, origins in leaves.items():
+            for s in origins[1::2]:
+                if not blocked[s]:
+                    kind[s] = "alt"
+                    for D in after(ch):
+                        pick(s, D, [h for h in idle if topo.mates(topo.chip(h), D) and reaches(h, D)
+                                    and topo.may_write(cores[s], h) and topo.die(h) == d])
+        for d, origins in leaves.items():
+            for s in origins:
+                if blocked[s]:
+                    spare = [h for h in idle if topo.chip(h) == ch and topo.die(h) == d]
+                    spare += [cores[r] for r in origins if kind[r] == "alt"]
+                    opts = {D: [h for h in spare if reaches(h, D)] for D in after(ch)}
+                    for D in sorted(after(ch), key=lambda D: len(opts[D])):
+                        pick(s, D, opts[D])
 
     prog = {}
 
-    def to_ranks(what, s, ranks, sets):
-        return [(cores[r], e, "arr%d" % s, what, r, "l", s, 1) for r, e in zip(ranks, sets)]
+    def to_ranks(what, s, src, ranks, sets):
+        return [(cores[r], e, "arr%d" % s, what, src, r, "l", s, 1) for r, e in zip(ranks, sets)]
 
     for s, c in enumerate(cores):
         ch = topo.chip(c)
-        A, B = after(ch)
+        A, B = [members[D] for D in after(ch)]
+        A0, A1 = A[:len(A) // 2], A[len(A) // 2:]
         peers = [r for r in members[ch] if r != s]
         on = engines(topo.mask(c, cores[peers[0]]))
-        if not blocked[s]:
-            off = engines(topo.mask(c, cores[members[A][0]]))
+        if kind[s] == "direct":
+            off = engines(topo.mask(c, cores[A[0]]))
             near = [e for e in on if e not in off]
-            both = members[A] + members[B]
             prog[c] = [
-                (["q0"], to_ranks("c", s, members[A], split(off, len(members[A])))),
-                (["q1", "q2"], to_ranks("s", s, both, split(off, len(both)))
-                 + to_ranks("s", s, peers, split(near, len(peers)))),
-                ([], to_ranks("c", s, members[B], split(off, len(members[B])))
-                 + to_ranks("c", s, peers, split(near, len(peers)))),
+                (["q0"], to_ranks("c", s, "x", A0, split(off, len(A0)))),
+                (["q1"], to_ranks("c", s, "x", A1, split(off, len(A1)))),
+                (["q2", "q3"], to_ranks("s", s, "x", A + B, split(off, len(A + B)))
+                 + to_ranks("s", s, "x", peers, split(near, len(peers)))),
+                ([], to_ranks("c", s, "x", B, split(off, len(B)))
+                 + to_ranks("c", s, "x", peers, split(near, len(peers)))),
             ]
         else:
-            far, near = on[:len(on) // 2], on[len(on) // 2:]
-
-            def hand(what, D, e):
-                h = route[(s, D)]
-                sem = "hs" if what == "s" else "hc%d" % jobs[h].index((s, D))
-                return (h, e, sem, what, members[D][0], "x", members[D][0], len(members[D]))
+            hA, hB = [route[(s, D)] for D in after(ch)]
+            far = [e for e in on if e in engines(topo.mask(c, hA)) and e in engines(topo.mask(c, hB))]
+            if len(far) == len(on):
+                far = on[:len(on) // 2]
+            near = [e for e in on if e not in far]
             two = split(far, 2)
+
+            def hand(what, h, sem, ranks, e):
+                return (h, e, sem, what, "x", ranks[0], "h", ranks[0], len(ranks))
             prog[c] = [
-                (["q0"], [hand("c", A, far)]),
-                (["q1"], [hand("c", B, far)]),
-                (["q2"], [hand("s", A, two[0]), hand("s", B, two[1])]
-                 + to_ranks("c", s, peers, split(near, len(peers)))),
-                ([], to_ranks("s", s, peers, split(near, len(peers)))),
+                (["q0"], [hand("c", hA, "hc0", A0, far)]),
+                (["q1"], [hand("c", hA, "hc1", A1, far)]),
+                (["q2"], [hand("s", hA, "hs", A, two[0]), hand("s", hB, "hs", B, two[1])]),
+                ([], [hand("c", hB, "hc0", B, far)]),
+                (["q3"], to_ranks("c", s, "x", peers, split(near, len(peers)))),
+                ([], to_ranks("s", s, "x", peers, split(near, len(peers)))),
             ]
-    for h, todo in jobs.items():
-        off = engines(topo.mask(h, cores[members[todo[0][1]][0]]))
-        every = [(s, r) for s, D in todo for r in members[D]]
-        calls = [(["hc0"], to_ranks("c", todo[0][0], members[todo[0][1]], split(off, len(members[todo[0][1]])))),
-                 (["hs"], [to_ranks("s", s, [r], [e])[0] for (s, r), e in zip(every, split(off, len(every)))])]
-        for i, (s, D) in enumerate(todo[1:]):
-            calls.append((["hc%d" % (i + 1)], to_ranks("c", s, members[D], split(off, len(members[D])))))
-        prog[h] = calls
+    for s, c in enumerate(cores):
+        if kind[s] != "direct":
+            A, B = [members[D] for D in after(topo.chip(c))]
+            A0, A1 = A[:len(A) // 2], A[len(A) // 2:]
+            hA, hB = [route[(s, D)] for D in after(topo.chip(c))]
+            off = engines(topo.mask(hA, cores[A[0]]))
+            prog.setdefault(hA, []).extend([
+                (["hc0"], to_ranks("c", s, "h", A0, split(off, len(A0)))),
+                (["hc1"], to_ranks("c", s, "h", A1, split(off, len(A1)))),
+                (["hs"], to_ranks("s", s, "h", A, split(off, len(A))))])
+            off = engines(topo.mask(hB, cores[B[0]]))
+            prog.setdefault(hB, []).extend([
+                (["hs"], to_ranks("s", s, "h", B, split(off, len(B)))),
+                (["hc0"], to_ranks("c", s, "h", B, split(off, len(B))))])
 
     inc = {}
     for c, calls in prog.items():
         for waits, trs in calls:
             for tr in trs:
                 inc[(tr[0], tr[2])] = inc.get((tr[0], tr[2]), 0) + len(tr[1])
-    return cores, members, after, blocked, prog, inc
+    return cores, members, after, kind, prog, inc
 
 
 def rank_program(g, core, T, topo):
-    cores, members, after, blocked, prog, inc = build(T, topo)
+    cores, members, after, kind, prog, inc = build(T, topo)
     if core not in prog:
         return
     me = T.rank_of(core)
+    codes = {"x": T.xq, "h": T.hq, "l": T.lq}
+    planes = {"x": T.xs, "h": T.hp, "l": T.ls}
 
     def cols(b, n=1, f=1):
         return slice(b * TW * f, (b + n) * TW * f)
@@ -132,17 +166,17 @@ def rank_program(g, core, T, topo):
         for name in waits:
             g.wait_ge(T.sem[name], inc.get((core, name), 1))
         call = []
-        for dst, engs, sem, what, sb, land, lb, n in trs:
+        for dst, engs, sem, what, sbuf, sb, lbuf, lb, n in trs:
             rid, pid = topo.addr(dst)[:2]
             mask = 0
             for e in engs:
                 mask |= 1 << e
             if what == "c":
-                src = T.xq[:, cols(sb, n)].bitcast(dt.uint8)
-                out = (T.lq if land == "l" else T.xq)[:, cols(lb, n)].bitcast(dt.uint8)
+                src = codes[sbuf][:, cols(sb, n)].bitcast(dt.uint8)
+                out = codes[lbuf][:, cols(lb, n)].bitcast(dt.uint8)
             else:
-                src = T.xs[:, cols(sb, n)]
-                out = (T.ls if land == "l" else T.xs)[:, cols(lb, n)]
+                src = planes[sbuf][:, cols(sb, n)]
+                out = planes[lbuf][:, cols(lb, n)]
             call.append(RemoteDMATransfer(dst_ids=[DstId(rid=rid, pnc=pid)], dma_engine_mask=mask,
                                           remote_sem=T.sem[sem], src=src, dst=out))
             sent += len(engs)
@@ -152,31 +186,32 @@ def rank_program(g, core, T, topo):
         return
 
     ch = topo.chip(core)
-    order = after(ch) + [ch]
-    queues = [g.sync, g.scalar]
-    for i, D in enumerate(order):
-        b, n = members[D][0], len(members[D])
-        queues[i % 2].dma_start(T.xb[:, cols(b, n, 4)], T.x[:, cols(b, n, 4)]).then_inc(T.sem["ld%d" % i], 16)
-    queues[len(order) % 2].dma_start(T.wb[:], T.w[:]).then_inc(T.sem.ldw, 16)
+    A, B = [members[D] for D in after(ch)]
+    half = len(A) // 2
+    loads = [(A[0], half), (A[half], len(A) - half), (B[0], len(B)), (members[ch][0], len(members[ch]))]
+    for i, (b, n) in enumerate(loads):
+        g.sync.dma_start(T.xb[:, cols(b, n, 4)], T.x[:, cols(b, n, 4)]).then_inc(T.sem["ld%d" % i], 16)
+    g.sync.dma_start(T.wb[:], T.w[:]).then_inc(T.sem.ldw, 16)
 
-    for i, D in enumerate(order):
-        b, n = members[D][0], len(members[D])
+    for i, (b, n) in enumerate(loads):
         g.vector.wait_ge(T.sem["ld%d" % i], 16)
         g.vector.quantize_mx(T.xq[:, cols(b, n)], T.xs[:, cols(b, n)], T.xb[:, cols(b, n, 4)]).then_inc(T.sem["q%d" % i], 1)
     g.vector.quantize_mx(T.lq[:, cols(me)], T.ls[:, cols(me)], T.xb[:, cols(me, 1, 4)]).then_inc(T.sem.qo, 1)
     g.vector.wait_ge(T.sem.ldw, 16)
     g.vector.quantize_mx(T.wq[:], T.ws[:], T.wb[:]).then_inc(T.sem.qw, 1)
 
+    due = ["direct", "alt", "hand"]
     pieces = [(members[ch][0], len(members[ch]))]
     for P in reversed(after(ch)):
         runs = []
         for j in members[P]:
-            if runs and blocked[runs[-1][0]] == blocked[j] and runs[-1][0] + runs[-1][1] == j:
+            if runs and kind[runs[-1][0]] == kind[j] and runs[-1][0] + runs[-1][1] == j:
                 runs[-1] = (runs[-1][0], runs[-1][1] + 1)
             else:
                 runs.append((j, 1))
-        pieces += sorted(runs, key=lambda r: blocked[r[0]])
+        pieces += sorted(runs, key=lambda r: due.index(kind[r[0]]))
 
+    queues = [g.sync, g.scalar]
     g.tensor.wait_ge(T.sem.qw, 1)
     stored = [0, 0]
     for k, (j0, n) in enumerate(pieces):

from concourse.bass import DstId, RemoteDMATransfer
from concourse.mybir import dt

N = 12
SIM = 64
TW = 128
BANK = 512
NP = 7
NL = 4

SCRATCH = {
    "xb": ("sbuf", [128, N * 4 * TW], "bfloat16"),
    "wb": ("sbuf", [128, 4 * TW], "bfloat16"),
    "xq": ("sbuf", [128, N * TW], "float8_e4m3fn_x4"),
    "xs": ("sbuf", [128, N * TW], "uint8"),
    "hq": ("sbuf", [128, N * TW], "float8_e4m3fn_x4"),
    "hp": ("sbuf", [128, N * TW], "uint8"),
    "wq": ("sbuf", [128, TW], "float8_e4m3fn_x4"),
    "ws": ("sbuf", [128, TW], "uint8"),
    "lq": ("sbuf", [128, N * TW], "float8_e4m3fn_x4"),
    "ls": ("sbuf", [128, N * TW], "uint8"),
    "ps": ("psum", [128, NP * BANK], "float32"),
    "yb": ("sbuf", [128, N * TW], "float32"),
}
SEMAPHORES = (["ldw", "qo", "qw", "st0", "st1", "sent", "hc0", "hc1", "hs"]
              + ["ld%d" % i for i in range(NL)] + ["q%d" % i for i in range(NL)]
              + ["arr%d" % j for j in range(N)] + ["mm%d" % k for k in range(NP)] + ["ev%d" % k for k in range(NP)])


def engines(mask):
    return [e for e in range(mask.bit_length()) if (mask >> e) & 1]


def split(engs, k):
    per = 1
    while per * 2 * k <= len(engs):
        per *= 2
    return [engs[i * per:(i + 1) * per] for i in range(k)]


def build(T, topo):
    cores = list(T.cores)
    chips = []
    for c in cores:
        if topo.chip(c) not in chips:
            chips.append(topo.chip(c))
    members = {ch: [r for r, c in enumerate(cores) if topo.chip(c) == ch] for ch in chips}

    def after(ch):
        i = chips.index(ch)
        return [chips[(i + k) % len(chips)] for k in range(1, len(chips))]

    def reaches(h, D):
        return all(topo.may_write(h, cores[r]) for r in members[D])

    idle = [h for h in range(SIM) if h not in cores]
    blocked = [any(not topo.may_write(c, d) for d in cores if d != c) for c in cores]
    kind = ["hand" if b else "direct" for b in blocked]
    route, used = {}, []

    def pick(s, D, opts):
        route[(s, D)] = [h for h in opts if h not in used][0]
        used.append(route[(s, D)])

    for ch in chips:
        leaves = {}
        for s in members[ch]:
            if blocked[s]:
                other = [topo.die(h) for h in idle if topo.chip(h) == ch and topo.die(h) != topo.die(cores[s])][0]
                leaves.setdefault(other, []).append(s)
        for s in members[ch]:
            if not blocked[s]:
                leaves.setdefault(topo.die(cores[s]), []).append(s)
        for d, origins in leaves.items():
            for s in origins[1::2]:
                if not blocked[s]:
                    kind[s] = "alt"
                    for D in after(ch):
                        pick(s, D, [h for h in idle if topo.mates(topo.chip(h), D) and reaches(h, D)
                                    and topo.may_write(cores[s], h) and topo.die(h) == d])
        for d, origins in leaves.items():
            for s in origins:
                if blocked[s]:
                    spare = [h for h in idle if topo.chip(h) == ch and topo.die(h) == d]
                    spare += [cores[r] for r in origins if kind[r] == "alt"]
                    opts = {D: [h for h in spare if reaches(h, D)] for D in after(ch)}
                    for D in sorted(after(ch), key=lambda D: len(opts[D])):
                        pick(s, D, opts[D])

    prog = {}

    def to_ranks(what, s, src, ranks, sets):
        return [(cores[r], e, "arr%d" % s, what, src, r, "l", s, 1) for r, e in zip(ranks, sets)]

    for s, c in enumerate(cores):
        ch = topo.chip(c)
        A, B = [members[D] for D in after(ch)]
        A0, A1 = A[:len(A) // 2], A[len(A) // 2:]
        peers = [r for r in members[ch] if r != s]
        on = engines(topo.mask(c, cores[peers[0]]))
        if kind[s] == "direct":
            off = engines(topo.mask(c, cores[A[0]]))
            near = [e for e in on if e not in off]
            prog[c] = [
                (["q0"], to_ranks("c", s, "x", A0, split(off, len(A0)))),
                (["q1"], to_ranks("c", s, "x", A1, split(off, len(A1)))),
                (["q2", "q3"], to_ranks("s", s, "x", A + B, split(off, len(A + B)))
                 + to_ranks("s", s, "x", peers, split(near, len(peers)))),
                ([], to_ranks("c", s, "x", B, split(off, len(B)))
                 + to_ranks("c", s, "x", peers, split(near, len(peers)))),
            ]
        else:
            hA, hB = [route[(s, D)] for D in after(ch)]
            far = [e for e in on if e in engines(topo.mask(c, hA)) and e in engines(topo.mask(c, hB))]
            if len(far) == len(on):
                far = on[:len(on) // 2]
            near = [e for e in on if e not in far]
            two = split(far, 2)

            def hand(what, h, sem, ranks, e):
                return (h, e, sem, what, "x", ranks[0], "h", ranks[0], len(ranks))
            prog[c] = [
                (["q0"], [hand("c", hA, "hc0", A0, far)]),
                (["q1"], [hand("c", hA, "hc1", A1, far)]),
                (["q2"], [hand("s", hA, "hs", A, two[0]), hand("s", hB, "hs", B, two[1])]),
                ([], [hand("c", hB, "hc0", B, far)]),
                (["q3"], to_ranks("c", s, "x", peers, split(near, len(peers)))),
                ([], to_ranks("s", s, "x", peers, split(near, len(peers)))),
            ]
    for s, c in enumerate(cores):
        if kind[s] != "direct":
            A, B = [members[D] for D in after(topo.chip(c))]
            A0, A1 = A[:len(A) // 2], A[len(A) // 2:]
            hA, hB = [route[(s, D)] for D in after(topo.chip(c))]
            off = engines(topo.mask(hA, cores[A[0]]))
            prog.setdefault(hA, []).extend([
                (["hc0"], to_ranks("c", s, "h", A0, split(off, len(A0)))),
                (["hc1"], to_ranks("c", s, "h", A1, split(off, len(A1)))),
                (["hs"], to_ranks("s", s, "h", A, split(off, len(A))))])
            off = engines(topo.mask(hB, cores[B[0]]))
            prog.setdefault(hB, []).extend([
                (["hs"], to_ranks("s", s, "h", B, split(off, len(B)))),
                (["hc0"], to_ranks("c", s, "h", B, split(off, len(B))))])

    inc = {}
    for c, calls in prog.items():
        for waits, trs in calls:
            for tr in trs:
                inc[(tr[0], tr[2])] = inc.get((tr[0], tr[2]), 0) + len(tr[1])
    return cores, members, after, kind, prog, inc


def rank_program(g, core, T, topo):
    cores, members, after, kind, prog, inc = build(T, topo)
    if core not in prog:
        return
    me = T.rank_of(core)
    codes = {"x": T.xq, "h": T.hq, "l": T.lq}
    planes = {"x": T.xs, "h": T.hp, "l": T.ls}

    def cols(b, n=1, f=1):
        return slice(b * TW * f, (b + n) * TW * f)

    sent = 0
    for waits, trs in prog[core]:
        for name in waits:
            g.wait_ge(T.sem[name], inc.get((core, name), 1))
        call = []
        for dst, engs, sem, what, sbuf, sb, lbuf, lb, n in trs:
            rid, pid = topo.addr(dst)[:2]
            mask = 0
            for e in engs:
                mask |= 1 << e
            if what == "c":
                src = codes[sbuf][:, cols(sb, n)].bitcast(dt.uint8)
                out = codes[lbuf][:, cols(lb, n)].bitcast(dt.uint8)
            else:
                src = planes[sbuf][:, cols(sb, n)]
                out = planes[lbuf][:, cols(lb, n)]
            call.append(RemoteDMATransfer(dst_ids=[DstId(rid=rid, pnc=pid)], dma_engine_mask=mask,
                                          remote_sem=T.sem[sem], src=src, dst=out))
            sent += len(engs)
        g.remote_dma_fused(call, local_sem=T.sem.sent)
    g.wait_ge(T.sem.sent, sent)
    if me is None:
        return

    ch = topo.chip(core)
    A, B = [members[D] for D in after(ch)]
    half = len(A) // 2
    loads = [(A[0], half), (A[half], len(A) - half), (B[0], len(B)), (members[ch][0], len(members[ch]))]
    for i, (b, n) in enumerate(loads):
        g.sync.dma_start(T.xb[:, cols(b, n, 4)], T.x[:, cols(b, n, 4)]).then_inc(T.sem["ld%d" % i], 16)
    g.sync.dma_start(T.wb[:], T.w[:]).then_inc(T.sem.ldw, 16)

    for i, (b, n) in enumerate(loads):
        g.vector.wait_ge(T.sem["ld%d" % i], 16)
        g.vector.quantize_mx(T.xq[:, cols(b, n)], T.xs[:, cols(b, n)], T.xb[:, cols(b, n, 4)]).then_inc(T.sem["q%d" % i], 1)
    g.vector.quantize_mx(T.lq[:, cols(me)], T.ls[:, cols(me)], T.xb[:, cols(me, 1, 4)]).then_inc(T.sem.qo, 1)
    g.vector.wait_ge(T.sem.ldw, 16)
    g.vector.quantize_mx(T.wq[:], T.ws[:], T.wb[:]).then_inc(T.sem.qw, 1)

    due = ["direct", "alt", "hand"]
    pieces = [(members[ch][0], len(members[ch]))]
    for P in reversed(after(ch)):
        runs = []
        for j in members[P]:
            if runs and kind[runs[-1][0]] == kind[j] and runs[-1][0] + runs[-1][1] == j:
                runs[-1] = (runs[-1][0], runs[-1][1] + 1)
            else:
                runs.append((j, 1))
        pieces += sorted(runs, key=lambda r: due.index(kind[r[0]]))

    queues = [g.sync, g.scalar]
    g.tensor.wait_ge(T.sem.qw, 1)
    stored = [0, 0]
    for k, (j0, n) in enumerate(pieces):
        for j in range(j0, j0 + n):
            if j == me:
                g.tensor.wait_ge(T.sem.qo, 1)
            else:
                g.tensor.wait_ge(T.sem["arr%d" % j], inc[(core, "arr%d" % j)])
        bank = T.ps[:, k * BANK:k * BANK + n * TW]
        g.tensor.matmul_mx(bank, T.wq[:], T.ws[:], T.lq[:, cols(j0, n)], T.ls[:, cols(j0, n)], True, True).then_inc(T.sem["mm%d" % k], 1)
        g.vector.wait_ge(T.sem["mm%d" % k], 1)
        g.vector.tensor_copy(T.yb[:, cols(j0, n)], bank).then_inc(T.sem["ev%d" % k], 1)
        q = queues[k % 2]
        q.wait_ge(T.sem["ev%d" % k], 1)
        q.dma_start(T.y[:, cols(j0, n)], T.yb[:, cols(j0, n)]).then_inc(T.sem["st%d" % (k % 2)], 16)
        stored[k % 2] += 16
    for i, q in enumerate(queues):
        q.wait_ge(T.sem["st%d" % i], stored[i])
